import numpy as np
import ml_dtypes


def mxq(x, axis, fmt="e4m3"):
    dtype, down = {"e4m3": (ml_dtypes.float8_e4m3fn, 7), "e5m2": (ml_dtypes.float8_e5m2, 14)}[fmt]
    v = np.moveaxis(np.asarray(x, np.float32).astype(ml_dtypes.bfloat16).astype(np.float64), axis, -1)
    blocks = v.reshape(v.shape[:-1] + (-1, 32))
    amax = np.abs(blocks).max(-1, keepdims=True)
    byte = np.maximum(np.where(amax > 0, np.frexp(amax)[1] - 1 + 127, 0) - down, 1)
    scale = np.exp2(byte - 127.0)
    codes = (blocks / scale).astype(np.float32).astype(dtype).astype(np.float64)
    return np.moveaxis((codes * scale).reshape(v.shape), -1, axis)


WIDE = False


def mx_kscale(k):
    if not WIDE:
        return np.ones(k)
    levels = np.array([10, -10, 5, -5, 0])
    if k % 512:
        return np.exp2(np.random.permutation(np.resize(levels, k // 32))).repeat(32)
    a = np.empty((k // 512, 16))
    for p in range(k // 512):
        a[p, :8] = np.random.permutation(np.resize(levels, 8))
        for g in range(8):
            far = levels[np.abs(levels - a[p, g]) >= 10]
            a[p, g + 8] = far[np.random.randint(len(far))]
    return np.exp2(a.ravel()).repeat(32)


def f64(x):
    return np.asarray(x).astype(np.float64)


def striped(idx):
    return np.tile(idx.reshape(-1, 16).T, (8, 1)).astype(np.uint16)


def unstriped(offs):
    return offs[:16].T.reshape(-1).astype(np.int64)


def pack_weight(w):
    k, n = w.shape
    w = f64(np.asarray(w, np.float32).astype(ml_dtypes.bfloat16)).reshape(k // 32, 32, n)
    amax = np.abs(w).max(1)
    byte = np.clip(np.where(amax > 0, np.frexp(amax)[1] - 1 + 127 - 7, 1), 1, 254)
    scaled = (w * np.exp2(127.0 - byte)[:, None, :]).reshape(k, n).astype(np.float32)
    words = np.ascontiguousarray(scaled.reshape(k // 512, 128, 4, n).transpose(0, 1, 3, 2)).astype(ml_dtypes.float8_e4m3fn).view(np.uint8)
    return words, np.ascontiguousarray(byte.astype(np.uint8).reshape(k // 512, 16, n))


def unpack_weight(words, scales):
    g, p, n, _ = words.shape
    vals = np.ascontiguousarray(words).view(ml_dtypes.float8_e4m3fn).astype(np.float64) * np.repeat(np.exp2(scales.astype(np.float64) - 127.0), 8, axis=1)[..., None]
    return vals.transpose(0, 1, 3, 2).reshape(g * 512, n)


K, T, S, V, N = 512, 4096, 2048, 512, 256


def setup_inputs():
    n = np.random.standard_normal
    s = mx_kscale(K)[:, None]
    packed_w1 = pack_weight(n((K, N)) / np.sqrt(K) / s)
    return {
        "xT": (n((K, T)) * s).astype(np.float32),
        "w1_words": packed_w1[0],
        "w1_scales": packed_w1[1],
        "offs": striped(np.random.permutation(T)[:S]),
    }


def reference(xT, w1_words, w1_scales, offs):
    xq = mxq(f64(xT)[:, unstriped(offs)], 0, "e4m3")
    e = np.exp(unpack_weight(w1_words, w1_scales).T @ xq)
    return np.log(e[:, :V] + e[:, V:2 * V] + e[:, 2 * V:3 * V] + e[:, 3 * V:4 * V])

@@ -1,0 +1,150 @@
+from contextlib import ExitStack
+
+import concourse.mybir as mybir
+
+K, T, S, V, N = 512, 4096, 2048, 512, 256
+FLOPS = 2 * K * N * S
+
+F32 = mybir.dt.float32
+BF16 = mybir.dt.bfloat16
+I32 = mybir.dt.int32
+U32 = mybir.dt.uint32
+U16 = mybir.dt.uint16
+U8 = mybir.dt.uint8
+FP8X4 = mybir.dt.float8_e4m3fn_x4
+ALU = mybir.AluOpType
+ACT = mybir.ActivationFunctionType
+
+P = 128
+PIECES = S // V
+ROW_TILES = N // P
+LIST_COLS = V // 16
+
+CHUNKS = (
+    ((1024, 1024), (1024, 0), (1024, 0), (1024, 0)),
+    ((1024, 1024), (1024, 1024), (1024, 0), (512, 512), (512, 160)),
+)
+COPIED = 2
+ON_GPSIMD = (2, 2)
+SUM_ORDER = ((3, 0, 1, 2), (3, 0, 2, 1))
+
+
+def tile_picked_lsep_none_e_kernel(tc, xT, w1_words, w1_scales, offs, out):
+    nc = tc.nc
+    with ExitStack() as ctx:
+        keep = ctx.enter_context(tc.tile_pool(name="keep", bufs=1))
+        psum = ctx.enter_context(tc.psum_pool(name="psum", bufs=1))
+
+        offsets = keep.tile([P, S // 16], U16, name="offsets")
+        w_codes = keep.tile([P, N], U32, name="w_codes", align_bytes=64)
+        w_scales = keep.tile([P, N], U8, name="w_scales", align_bytes=64)
+        nc.gpsimd.memset(w_scales[:], 0)
+
+        x_rows = xT.rearrange("(p j) t -> p j t", j=4)
+        picked = [keep.tile([P, 2, V], U32, name=f"picked{d}") for d in range(PIECES)]
+        for u in range(2):
+            window = keep.tile([P, 2 * T], BF16, name=f"window{u}", align_bytes=64)
+            pairs = window[:].rearrange("p (t e) -> p t e", e=2)
+            t0 = 0
+            for c, (width, on_scalar) in enumerate(CHUNKS[u]):
+                raw = keep.tile([P, 2, width], F32, name=f"raw{u}_{c}")
+                nc.sync.dma_start(out=raw[:], in_=x_rows[:, 2 * u : 2 * u + 2, t0 : t0 + width])
+                turned = raw[:].rearrange("p e t -> p t e")
+                if on_scalar > 0:
+                    nc.scalar.activation(pairs[:, t0 : t0 + on_scalar, :], turned[:, :on_scalar, :], ACT.Copy)
+                if on_scalar < width:
+                    nc.vector.tensor_copy(pairs[:, t0 + on_scalar : t0 + width, :], turned[:, on_scalar:, :])
+                t0 += width
+            if u == 0:
+                nc.sync.dma_start(offsets[:], offs)
+            words = window[:].bitcast(U32)
+            for d in range(PIECES):
+                nc.vector.tensor_copy(
+                    picked[d][:, u, :], words.indirect(offsets[:, d * LIST_COLS : (d + 1) * LIST_COLS])
+                )
+
+        nc.sync.dma_start(
+            out=w_codes[:].bitcast(I32), in_=w1_words[0].rearrange("p n t -> p (n t)").bitcast(I32)
+        )
+        for q in range(4):
+            nc.sync.dma_start(
+                out=w_scales[32 * q : 32 * q + 4, :].bitcast(I32), in_=w1_scales[0, 4 * q : 4 * q + 4, :].bitcast(I32)
+            )
+
+        y = {}
+        for d in range(PIECES):
+            woven = keep.tile([P, 4 * V], BF16, name=f"woven{d}", align_bytes=64)
+            nc.scalar.copy(
+                woven[:].bitcast(U32).rearrange("p (n u) -> p n u", u=2), picked[d][:].rearrange("p u n -> p n u")
+            )
+            codes = keep.tile([P, V], U32, name=f"codes{d}", align_bytes=64)
+            scales = keep.tile([P, V], U8, name=f"scales{d}", align_bytes=64)
+            nc.vector.quantize_mx(out=codes[:].bitcast(FP8X4), scales=scales[:], in_=woven[:])
+            for r in range(ROW_TILES):
+                y[d, r] = psum.tile([P, V], F32, name=f"y{d}_{r}")
+                nc.tensor.matmul_mx(
+                    out=y[d, r][:],
+                    lhsT=w_codes[:, r * P : (r + 1) * P].bitcast(FP8X4),
+                    lhsT_scale=w_scales[:, r * P : (r + 1) * P],
+                    rhs=codes[:].bitcast(FP8X4),
+                    rhs_scale=scales[:],
+                    start=True,
+                    stop=True,
+                )
+
+        def fresh(name):
+            return keep.tile([P, V], F32, name=name)
+
+        in_sbuf = {}
+        for r in range(ROW_TILES):
+            for d in range(COPIED):
+                in_sbuf[d, r] = fresh(f"y_copy{d}_{r}")
+                nc.scalar.activation(in_sbuf[d, r][:], y[d, r][:], ACT.Copy)
+
+        largest = {}
+        term = {}
+
+        def exp_term(d, r):
+            gap = fresh(f"gap{d}_{r}")
+            if d < ON_GPSIMD[r]:
+                nc.gpsimd.tensor_tensor(gap[:], in_sbuf[d, r][:], largest[r][:], ALU.subtract)
+            else:
+                nc.vector.tensor_tensor(gap[:], y[d, r][:], largest[r][:], ALU.subtract)
+            term[d, r] = fresh(f"term{d}_{r}")
+            nc.scalar.activation(term[d, r][:], gap[:], ACT.Exp)
+
+        def find_largest(r):
+            top = in_sbuf[0, r]
+            for d in range(1, PIECES):
+                higher = fresh(f"top{d}_{r}")
+                nc.vector.tensor_tensor(higher[:], y[d, r][:], top[:], ALU.max)
+                top = higher
+            largest[r] = top
+
+        find_largest(0)
+        exp_term(3, 0)
+        exp_term(0, 0)
+        find_largest(1)
+        exp_term(1, 0)
+        exp_term(2, 0)
+        exp_term(3, 1)
+        exp_term(0, 1)
+        exp_term(2, 1)
+        exp_term(1, 1)
+
+        sums = {}
+        for r in range(ROW_TILES):
+            acc = term[SUM_ORDER[r][0], r]
+            for d in SUM_ORDER[r][1:]:
+                more = fresh(f"sum{d}_{r}")
+                nc.vector.tensor_tensor(more[:], acc[:], term[d, r][:], ALU.add)
+                acc = more
+            sums[r] = acc
+        for r in range(ROW_TILES):
+            for h in range(2):
+                cols = slice(h * (V // 2), (h + 1) * (V // 2))
+                logged = keep.tile([P, V // 2], F32, name=f"logged{r}_{h}")
+                nc.scalar.activation(logged[:], sums[r][:, cols], ACT.Ln)
+                result = keep.tile([P, V // 2], F32, name=f"result{r}_{h}")
+                nc.vector.tensor_tensor(result[:], logged[:], largest[r][:, cols], ALU.add)
+                nc.sync.dma_start(out=out[r * P : (r + 1) * P, cols], in_=result[:])

@@ -1,6 +1,7 @@
 from contextlib import ExitStack
 
 import concourse.mybir as mybir
+from concourse.masks import make_identity
 
 K, T, S, V, N = 512, 4096, 2048, 512, 256
 FLOPS = 2 * K * N * S
@@ -24,9 +25,9 @@ CHUNKS = (
     ((1024, 1024), (1024, 0), (1024, 0), (1024, 0)),
     ((1024, 1024), (1024, 1024), (1024, 0), (512, 512), (512, 160)),
 )
-COPIED = 2
-ON_GPSIMD = (2, 2)
-SUM_ORDER = ((3, 0, 1, 2), (3, 0, 2, 1))
+int_of = {"0": 0, "1": 1, "2": 2, "3": 3}
+BANK_OF = ((0, 1), (0, 1))
+ORDER = "c0_00 c0_10 n1_00 n1_01 n1_10 c1_00 c1_10 n2_00 n2_01 n3_00 T_00 eP_00 n3_01 T_01 eP_01 s3_00 e3_00 s2_00 e2_00 n2_10 s2_01 e2_01 s3_01 e3_01 n3_10 T_10 eP_10 n1_11 s2_10 e2_10 n2_11 s3_10 e3_10 n3_11 T_11 eP_11 s3_11 e3_11 s2_11 e2_11 B_00 B_01 B_10 B_11 a1_00 a1_01 a1_10 a2_00 a2_01 a1_11 a2_10 a2_11 ln_00 ln_01 f_00 ln_10 f_01 ln_11 f_10 f_11"
 
 
 def tile_picked_lsep_none_e_kernel(tc, xT, w1_words, w1_scales, offs, out):
@@ -39,6 +40,9 @@ def tile_picked_lsep_none_e_kernel(tc, xT, w1_words, w1_scales, offs, out):
         w_codes = keep.tile([P, N], U32, name="w_codes", align_bytes=64)
         w_scales = keep.tile([P, N], U8, name="w_scales", align_bytes=64)
         nc.gpsimd.memset(w_scales[:], 0)
+
+        ident = keep.tile([P, P], F32, name="ident")
+        make_identity(nc, ident[:])
 
         x_rows = xT.rearrange("(p j) t -> p j t", j=4)
         picked = [keep.tile([P, 2, V], U32, name=f"picked{d}") for d in range(PIECES)]
@@ -92,59 +96,65 @@ def tile_picked_lsep_none_e_kernel(tc, xT, w1_words, w1_scales, offs, out):
                     stop=True,
                 )
 
-        def fresh(name):
-            return keep.tile([P, V], F32, name=name)
+        half = V // 2
+        made = {}
+        minus_one = keep.tile([P, 1], F32, name="minus_one", tag="exp_then_ln")
+        nc.gpsimd.memset(minus_one[:], -1.0)
 
-        in_sbuf = {}
-        for r in range(ROW_TILES):
-            for d in range(COPIED):
-                in_sbuf[d, r] = fresh(f"y_copy{d}_{r}")
-                nc.scalar.activation(in_sbuf[d, r][:], y[d, r][:], ACT.Copy)
+        def fresh(key, width):
+            made[key] = keep.tile([P, width], F32, name=key)
+            return made[key][:]
 
-        largest = {}
-        term = {}
-
-        def exp_term(d, r):
-            gap = fresh(f"gap{d}_{r}")
-            if d < ON_GPSIMD[r]:
-                nc.gpsimd.tensor_tensor(gap[:], in_sbuf[d, r][:], largest[r][:], ALU.subtract)
+        def step(kind, r, h):
+            cols = slice(h * half, (h + 1) * half)
+            q = f"{r}{h}"
+            bank = y[BANK_OF[r][h], r]
+            if kind == "c0" or kind == "c1":
+                d = int_of[kind[1]]
+                nc.scalar.activation(fresh(f"neg{d}_{r}", V), y[d, r][:], ACT.Copy, scale=-1.0)
+            elif kind == "n1":
+                nc.vector.scalar_tensor_tensor(
+                    fresh("n1" + q, half), made[f"neg0_{r}"][:, cols], -1.0, y[1, r][:, cols], ALU.mult, ALU.max
+                )
+            elif kind == "n2" or kind == "n3":
+                d = int_of[kind[1]]
+                nc.vector.tensor_tensor(fresh(kind + q, half), y[d, r][:, cols], made[f"n{d - 1}" + q][:], ALU.max)
+            elif kind == "s2" or kind == "s3":
+                d = int_of[kind[1]]
+                nc.vector.tensor_tensor(fresh(kind + q, half), made["n3" + q][:], y[d, r][:, cols], ALU.subtract)
+            elif kind == "e2" or kind == "e3":
+                nc.scalar.activation(fresh(kind + q, half), made["s" + kind[1] + q][:], ACT.Exp, scale=minus_one[:])
+            elif kind == "T":
+                for d in range(2):
+                    for b in range(2):
+                        to = bank[:, (2 * d + b) * P : (2 * d + b + 1) * P]
+                        src = made[f"neg{d}_{r}"][:, h * half + b * P : h * half + (b + 1) * P]
+                        nc.tensor.matmul(to, src, ident[:], start=True, stop=False, is_transpose=True)
+                        top = made["n3" + q][:, b * P : (b + 1) * P]
+                        nc.tensor.matmul(to, top, ident[:], start=False, stop=True, is_transpose=True)
+            elif kind == "eP":
+                nc.scalar.activation(fresh("eP" + q, V), bank[:], ACT.Exp, scale=minus_one[:])
+            elif kind == "B":
+                for b in range(2):
+                    for d in range(2):
+                        src = made["eP" + q][:, (2 * d + b) * P : (2 * d + b + 1) * P]
+                        nc.tensor.matmul(
+                            bank[:, b * P : (b + 1) * P], src, ident[:], start=d == 0, stop=d == 1, is_transpose=True
+                        )
+            elif kind == "a1":
+                nc.vector.tensor_tensor(fresh("a1" + q, half), made["e2" + q][:], made["e3" + q][:], ALU.add)
+            elif kind == "a2":
+                nc.vector.tensor_tensor(fresh("a2" + q, half), bank[:, :half], made["a1" + q][:], ALU.add)
+            elif kind == "ln":
+                if "logged" not in made:
+                    made["logged"] = keep.tile([P, 4 * half], F32, name="logged", tag="exp_then_ln")
+                slot = 2 * r + h
+                made["ln" + q] = made["logged"][:, slot * half : (slot + 1) * half]
+                nc.scalar.activation(made["ln" + q], made["a2" + q][:], ACT.Ln)
             else:
-                nc.vector.tensor_tensor(gap[:], y[d, r][:], largest[r][:], ALU.subtract)
-            term[d, r] = fresh(f"term{d}_{r}")
-            nc.scalar.activation(term[d, r][:], gap[:], ACT.Exp)
+                nc.vector.tensor_tensor(fresh("f" + q, half), made["ln" + q][:], made["n3" + q][:], ALU.add)
+                nc.sync.dma_start(out=out[r * P : (r + 1) * P, cols], in_=made["f" + q][:])
 
-        def find_largest(r):
-            top = in_sbuf[0, r]
-            for d in range(1, PIECES):
-                higher = fresh(f"top{d}_{r}")
-                nc.vector.tensor_tensor(higher[:], y[d, r][:], top[:], ALU.max)
-                top = higher
-            largest[r] = top
-
-        find_largest(0)
-        exp_term(3, 0)
-        exp_term(0, 0)
-        find_largest(1)
-        exp_term(1, 0)
-        exp_term(2, 0)
-        exp_term(3, 1)
-        exp_term(0, 1)
-        exp_term(2, 1)
-        exp_term(1, 1)
-
-        sums = {}
-        for r in range(ROW_TILES):
-            acc = term[SUM_ORDER[r][0], r]
-            for d in SUM_ORDER[r][1:]:
-                more = fresh(f"sum{d}_{r}")
-                nc.vector.tensor_tensor(more[:], acc[:], term[d, r][:], ALU.add)
-                acc = more
-            sums[r] = acc
-        for r in range(ROW_TILES):
-            for h in range(2):
-                cols = slice(h * (V // 2), (h + 1) * (V // 2))
-                logged = keep.tile([P, V // 2], F32, name=f"logged{r}_{h}")
-                nc.scalar.activation(logged[:], sums[r][:, cols], ACT.Ln)
-                result = keep.tile([P, V // 2], F32, name=f"result{r}_{h}")
-                nc.vector.tensor_tensor(result[:], logged[:], largest[r][:, cols], ALU.add)
-                nc.sync.dma_start(out=out[r * P : (r + 1) * P, cols], in_=result[:])
+        for item in ORDER.split():
+            kind, where = item.split("_")
+            step(kind, int_of[where[0]], int_of[where[1]])

@@ -22,12 +22,13 @@ ROW_TILES = N // P
 LIST_COLS = V // 16
 
 CHUNKS = (
-    ((1024, 1024), (1024, 0), (1024, 0), (1024, 0)),
-    ((1024, 1024), (1024, 1024), (1024, 0), (512, 512), (512, 160)),
+    ((3072, 1024), (1024, 384)),
+    ((2048, 1280), (1024, 0), (512, 256), (512, 160)),
 )
+OUT_WIDTHS = (256, 256, 256, 128, 128)
 int_of = {"0": 0, "1": 1, "2": 2, "3": 3}
 BANK_OF = ((0, 1), (0, 1))
-ORDER = "c0_00 c0_10 n1_00 n1_01 n1_10 c1_00 c1_10 n2_00 n2_01 n3_00 T_00 eP_00 n3_01 T_01 eP_01 s3_00 e3_00 s2_00 e2_00 n2_10 s2_01 e2_01 s3_01 e3_01 n3_10 T_10 eP_10 n1_11 s2_10 e2_10 n2_11 s3_10 e3_10 n3_11 T_11 eP_11 s3_11 e3_11 s2_11 e2_11 B_00 B_01 B_10 B_11 a1_00 a1_01 a1_10 a2_00 a2_01 a1_11 a2_10 a2_11 ln_00 ln_01 f_00 ln_10 f_01 ln_11 f_10 f_11"
+ORDER = "c0_00 c0_10 n1_00 n1_01 n1_10 c1_00 c1_10 n2_00 n2_01 n3_00 U_00 U_01 T_00 n3_01 T_01 s2_00 e2_00 s3_00 e3_00 s2_01 e2_01 eP_00 eP_01 n2_10 n1_11 n3_10 U_10 T_10 n2_11 s3_01 e3_01 s3_10 e3_10 eP_10 n3_11 U_11 B_00 T_11 s2_10 e2_10 s3_11 e3_11 a1_00 s2_11 e2_11 eP_11 a2_00 B_01 B_10 B_11 a1_01 a1_10 a1_11 a2_01 a2_10 a2_11"
 
 
 def tile_picked_lsep_none_e_kernel(tc, xT, w1_words, w1_scales, offs, out):
@@ -98,6 +99,7 @@ def tile_picked_lsep_none_e_kernel(tc, xT, w1_words, w1_scales, offs, out):
 
         half = V // 2
         made = {}
+        pair_sums = keep.tile([P, 4 * half], F32, name="pair_sums", tag="sums_then_results")
         minus_one = keep.tile([P, 1], F32, name="minus_one", tag="exp_then_ln")
         nc.gpsimd.memset(minus_one[:], -1.0)
 
@@ -124,14 +126,18 @@ def tile_picked_lsep_none_e_kernel(tc, xT, w1_words, w1_scales, offs, out):
                 nc.vector.tensor_tensor(fresh(kind + q, half), made["n3" + q][:], y[d, r][:, cols], ALU.subtract)
             elif kind == "e2" or kind == "e3":
                 nc.scalar.activation(fresh(kind + q, half), made["s" + kind[1] + q][:], ACT.Exp, scale=minus_one[:])
+            elif kind == "U":
+                for j in range(4):
+                    src = made[f"neg{j // 2}_{r}"][:, h * half + j % 2 * P : h * half + (j % 2 + 1) * P]
+                    nc.tensor.matmul(
+                        bank[:, j * P : (j + 1) * P], src, ident[:], start=j == 0, stop=False, is_transpose=True
+                    )
             elif kind == "T":
-                for d in range(2):
-                    for b in range(2):
-                        to = bank[:, (2 * d + b) * P : (2 * d + b + 1) * P]
-                        src = made[f"neg{d}_{r}"][:, h * half + b * P : h * half + (b + 1) * P]
-                        nc.tensor.matmul(to, src, ident[:], start=True, stop=False, is_transpose=True)
-                        top = made["n3" + q][:, b * P : (b + 1) * P]
-                        nc.tensor.matmul(to, top, ident[:], start=False, stop=True, is_transpose=True)
+                for j in range(4):
+                    top = made["n3" + q][:, j % 2 * P : (j % 2 + 1) * P]
+                    nc.tensor.matmul(
+                        bank[:, j * P : (j + 1) * P], top, ident[:], start=False, stop=j == 3, is_transpose=True
+                    )
             elif kind == "eP":
                 nc.scalar.activation(fresh("eP" + q, V), bank[:], ACT.Exp, scale=minus_one[:])
             elif kind == "B":
@@ -142,19 +148,26 @@ def tile_picked_lsep_none_e_kernel(tc, xT, w1_words, w1_scales, offs, out):
                             bank[:, b * P : (b + 1) * P], src, ident[:], start=d == 0, stop=d == 1, is_transpose=True
                         )
             elif kind == "a1":
-                nc.vector.tensor_tensor(fresh("a1" + q, half), made["e2" + q][:], made["e3" + q][:], ALU.add)
-            elif kind == "a2":
-                nc.vector.tensor_tensor(fresh("a2" + q, half), bank[:, :half], made["a1" + q][:], ALU.add)
-            elif kind == "ln":
-                if "logged" not in made:
-                    made["logged"] = keep.tile([P, 4 * half], F32, name="logged", tag="exp_then_ln")
-                slot = 2 * r + h
-                made["ln" + q] = made["logged"][:, slot * half : (slot + 1) * half]
-                nc.scalar.activation(made["ln" + q], made["a2" + q][:], ACT.Ln)
+                made["a1" + q] = pair_sums[:, (2 * r + h) * half : (2 * r + h + 1) * half]
+                nc.vector.tensor_tensor(made["a1" + q], made["e2" + q][:], made["e3" + q][:], ALU.add)
             else:
-                nc.vector.tensor_tensor(fresh("f" + q, half), made["ln" + q][:], made["n3" + q][:], ALU.add)
-                nc.sync.dma_start(out=out[r * P : (r + 1) * P, cols], in_=made["f" + q][:])
+                nc.vector.tensor_tensor(fresh("a2" + q, half), bank[:, :half], made["a1" + q][:], ALU.add)
 
         for item in ORDER.split():
             kind, where = item.split("_")
             step(kind, int_of[where[0]], int_of[where[1]])
+
+        logged = keep.tile([P, ROW_TILES * V], F32, name="logged", tag="exp_then_ln")
+        result = keep.tile([P, ROW_TILES * V], F32, name="result", tag="sums_then_results")
+        c0 = 0
+        for width in OUT_WIDTHS:
+            r, h, inner = c0 // V, c0 % V // half, slice(c0 % half, c0 % half + width)
+            q = f"{r}{h}"
+            nc.scalar.activation(logged[:, c0 : c0 + width], made["a2" + q][:, inner], ACT.Ln)
+            nc.vector.tensor_tensor(
+                result[:, c0 : c0 + width], logged[:, c0 : c0 + width], made["n3" + q][:, inner], ALU.add
+            )
+            nc.sync.dma_start(
+                out=out[r * P : (r + 1) * P, c0 % V : c0 % V + width], in_=result[:, c0 : c0 + width]
+            )
+            c0 += width

@@ -22,8 +22,8 @@ ROW_TILES = N // P
 LIST_COLS = V // 16
 
 CHUNKS = (
-    ((3072, 1024), (1024, 384)),
-    ((2048, 1280), (1024, 0), (512, 256), (512, 160)),
+    ((3072, 1280), (1024, 384)),
+    ((1536, 1536), (1536, 512), (512, 192), (512, 160)),
 )
 OUT_WIDTHS = (256, 256, 256, 128, 128)
 int_of = {"0": 0, "1": 1, "2": 2, "3": 3}

@@ -17,18 +17,29 @@ ALU = mybir.AluOpType
 ACT = mybir.ActivationFunctionType
 
 P = 128
+PACK = 4
 PIECES = S // V
 ROW_TILES = N // P
+HALF = V // 2
 LIST_COLS = V // 16
 
-CHUNKS = (
+LOADS = (
     ((3072, 1280), (1024, 384)),
     ((1536, 1536), (1536, 512), (512, 192), (512, 160)),
 )
-OUT_WIDTHS = (256, 256, 256, 128, 128)
-int_of = {"0": 0, "1": 1, "2": 2, "3": 3}
-BANK_OF = ((0, 1), (0, 1))
-ORDER = "c0_00 c0_10 n1_00 n1_01 n1_10 c1_00 c1_10 n2_00 n2_01 n3_00 U_00 U_01 T_00 n3_01 T_01 s2_00 e2_00 s3_00 e3_00 s2_01 e2_01 eP_00 eP_01 n2_10 n1_11 n3_10 U_10 T_10 n2_11 s3_01 e3_01 s3_10 e3_10 eP_10 n3_11 U_11 B_00 T_11 s2_10 e2_10 s3_11 e3_11 a1_00 s2_11 e2_11 eP_11 a2_00 B_01 B_10 B_11 a1_01 a1_10 a1_11 a2_01 a2_10 a2_11"
+
+STEPS = """
+gather:0 weave:00 weave:01 gather:1 weave:10 weave:11 gather:2 weave:20 weave:21 quantise:00 score:00
+quantise:01 score:01 quantise:10 score:10 quantise:11 score:11 negate:00 gather:3 weave:30 weave:31
+quantise:20 score:20 quantise:21 score:21 max1:00 max1:10 negate:10 quantise:30 score:30 max2:00
+quantise:31 score:31 max2:10 negate:01 negate:11 max3:00 max3:10 gap2:00 exp2:00 gap2:10 exp2:10 max1:01
+gap3:00 exp3:00 max2:01 max1:11 turn_scores:00 turn_scores:10 turn_max:00 exp01:00 turn_max:10 exp01:10
+max3:01 gap3:10 exp3:10 max2:11 gap2:01 exp2:01 turn_scores:01 turn_max:01 exp01:01 turn_scores:11
+max3:11 gap3:01 exp3:01 sum01:00 sum01:10 gap2:11 exp2:11 gap3:11 turn_max:11 exp01:11 exp3:11 sum23:00
+sum23:10 total:00 sum01:01 sum01:11 sum23:01 total:10 sum23:11 total:01 total:11
+"""
+
+STORES = ((0, 0, 0, HALF), (1, 0, 0, HALF), (0, 1, 0, HALF), (1, 1, 0, P), (1, 1, P, P))
 
 
 def tile_picked_lsep_none_e_kernel(tc, xT, w1_words, w1_scales, offs, out):
@@ -41,133 +52,159 @@ def tile_picked_lsep_none_e_kernel(tc, xT, w1_words, w1_scales, offs, out):
         w_codes = keep.tile([P, N], U32, name="w_codes", align_bytes=64)
         w_scales = keep.tile([P, N], U8, name="w_scales", align_bytes=64)
         nc.gpsimd.memset(w_scales[:], 0)
-
         ident = keep.tile([P, P], F32, name="ident")
         make_identity(nc, ident[:])
 
-        x_rows = xT.rearrange("(p j) t -> p j t", j=4)
-        picked = [keep.tile([P, 2, V], U32, name=f"picked{d}") for d in range(PIECES)]
+        shared = keep.tile([P, 3, V], U32, name="picked13")
+        picked = {1: shared[:, 1:3, :], 3: shared[:, 0:2, :]}
+        for d in (0, 2):
+            picked[d] = keep.tile([P, 2, V], U32, name=f"picked{d}")[:]
+
+        def gather_pair(u, d):
+            entries = offsets[:, d * LIST_COLS : (d + 1) * LIST_COLS]
+            nc.vector.tensor_copy(picked[d][:, u, :], windows[u][:].bitcast(U32).indirect(entries))
+
+        x_rows = xT.rearrange("(p j) t -> p j t", j=PACK)
+        windows = []
         for u in range(2):
-            window = keep.tile([P, 2 * T], BF16, name=f"window{u}", align_bytes=64)
-            pairs = window[:].rearrange("p (t e) -> p t e", e=2)
+            windows.append(keep.tile([P, 2 * T], BF16, name=f"window{u}", align_bytes=64))
+            pairs = windows[u][:].rearrange("p (t e) -> p t e", e=2)
             t0 = 0
-            for c, (width, on_scalar) in enumerate(CHUNKS[u]):
+            for c, (width, on_scalar) in enumerate(LOADS[u]):
                 raw = keep.tile([P, 2, width], F32, name=f"raw{u}_{c}")
                 nc.sync.dma_start(out=raw[:], in_=x_rows[:, 2 * u : 2 * u + 2, t0 : t0 + width])
-                turned = raw[:].rearrange("p e t -> p t e")
-                if on_scalar > 0:
-                    nc.scalar.activation(pairs[:, t0 : t0 + on_scalar, :], turned[:, :on_scalar, :], ACT.Copy)
+                by_token = raw[:].rearrange("p e t -> p t e")
+                nc.scalar.activation(pairs[:, t0 : t0 + on_scalar, :], by_token[:, :on_scalar, :], ACT.Copy)
                 if on_scalar < width:
-                    nc.vector.tensor_copy(pairs[:, t0 + on_scalar : t0 + width, :], turned[:, on_scalar:, :])
+                    nc.vector.tensor_copy(pairs[:, t0 + on_scalar : t0 + width, :], by_token[:, on_scalar:, :])
                 t0 += width
             if u == 0:
                 nc.sync.dma_start(offsets[:], offs)
-            words = window[:].bitcast(U32)
-            for d in range(PIECES):
-                nc.vector.tensor_copy(
-                    picked[d][:, u, :], words.indirect(offsets[:, d * LIST_COLS : (d + 1) * LIST_COLS])
-                )
+                for d in range(PIECES):
+                    gather_pair(0, d)
 
-        nc.sync.dma_start(
-            out=w_codes[:].bitcast(I32), in_=w1_words[0].rearrange("p n t -> p (n t)").bitcast(I32)
-        )
+        nc.sync.dma_start(out=w_codes[:].bitcast(I32), in_=w1_words[0].rearrange("p n t -> p (n t)").bitcast(I32))
         for q in range(4):
             nc.sync.dma_start(
                 out=w_scales[32 * q : 32 * q + 4, :].bitcast(I32), in_=w1_scales[0, 4 * q : 4 * q + 4, :].bitcast(I32)
             )
 
-        y = {}
-        for d in range(PIECES):
-            woven = keep.tile([P, 4 * V], BF16, name=f"woven{d}", align_bytes=64)
-            nc.scalar.copy(
-                woven[:].bitcast(U32).rearrange("p (n u) -> p n u", u=2), picked[d][:].rearrange("p u n -> p n u")
-            )
-            codes = keep.tile([P, V], U32, name=f"codes{d}", align_bytes=64)
-            scales = keep.tile([P, V], U8, name=f"scales{d}", align_bytes=64)
-            nc.vector.quantize_mx(out=codes[:].bitcast(FP8X4), scales=scales[:], in_=woven[:])
+        minus_one = keep.tile([P, 1], F32, name="minus_one", tag="exp_then_ln")
+        nc.gpsimd.memset(minus_one[:], -1.0)
+        sums23 = keep.tile([P, ROW_TILES * V], F32, name="sums23", tag="sums_then_results")
+
+        made = {}
+
+        def fresh(name, i, j, width, dtype=F32):
+            made[name, i, j] = keep.tile([P, width], dtype, name=f"{name}_{i}{j}", align_bytes=64)[:]
+            return made[name, i, j]
+
+        def scores(d, r, h):
+            return made["bank", d, h][:, r * HALF : (r + 1) * HALF]
+
+        def turn(to, src, start, stop):
+            nc.tensor.matmul(to, src, ident[:], start=start, stop=stop, is_transpose=True)
+
+        def weave(d, h):
+            woven = fresh("woven", d, h, PACK * HALF, BF16).bitcast(U32).rearrange("p (n u) -> p n u", u=2)
+            nc.scalar.copy(woven, picked[d][:, :, h * HALF : (h + 1) * HALF].rearrange("p u n -> p n u"))
+
+        def quantise(d, h):
+            codes = fresh("codes", d, h, HALF, U32)
+            nc.vector.quantize_mx(out=codes.bitcast(FP8X4), scales=fresh("scales", d, h, HALF, U8), in_=made["woven", d, h])
+
+        def score(d, h):
+            made["bank", d, h] = psum.tile([P, V], F32, name=f"bank{d}{h}")[:]
             for r in range(ROW_TILES):
-                y[d, r] = psum.tile([P, V], F32, name=f"y{d}_{r}")
                 nc.tensor.matmul_mx(
-                    out=y[d, r][:],
+                    out=scores(d, r, h),
                     lhsT=w_codes[:, r * P : (r + 1) * P].bitcast(FP8X4),
                     lhsT_scale=w_scales[:, r * P : (r + 1) * P],
-                    rhs=codes[:].bitcast(FP8X4),
-                    rhs_scale=scales[:],
+                    rhs=made["codes", d, h].bitcast(FP8X4),
+                    rhs_scale=made["scales", d, h],
                     start=True,
                     stop=True,
                 )
 
-        half = V // 2
-        made = {}
-        pair_sums = keep.tile([P, 4 * half], F32, name="pair_sums", tag="sums_then_results")
-        minus_one = keep.tile([P, 1], F32, name="minus_one", tag="exp_then_ln")
-        nc.gpsimd.memset(minus_one[:], -1.0)
+        def negate(d, h):
+            nc.scalar.activation(fresh("negated", d, h, V), made["bank", d, h], ACT.Copy, scale=-1.0)
 
-        def fresh(key, width):
-            made[key] = keep.tile([P, width], F32, name=key)
-            return made[key][:]
+        def max1(r, h):
+            minus_y0 = made["negated", 0, h][:, r * HALF : (r + 1) * HALF]
+            nc.vector.scalar_tensor_tensor(fresh("max1", r, h, HALF), minus_y0, -1.0, scores(1, r, h), ALU.mult, ALU.max)
 
-        def step(kind, r, h):
-            cols = slice(h * half, (h + 1) * half)
-            q = f"{r}{h}"
-            bank = y[BANK_OF[r][h], r]
-            if kind == "c0" or kind == "c1":
-                d = int_of[kind[1]]
-                nc.scalar.activation(fresh(f"neg{d}_{r}", V), y[d, r][:], ACT.Copy, scale=-1.0)
-            elif kind == "n1":
-                nc.vector.scalar_tensor_tensor(
-                    fresh("n1" + q, half), made[f"neg0_{r}"][:, cols], -1.0, y[1, r][:, cols], ALU.mult, ALU.max
-                )
-            elif kind == "n2" or kind == "n3":
-                d = int_of[kind[1]]
-                nc.vector.tensor_tensor(fresh(kind + q, half), y[d, r][:, cols], made[f"n{d - 1}" + q][:], ALU.max)
-            elif kind == "s2" or kind == "s3":
-                d = int_of[kind[1]]
-                nc.vector.tensor_tensor(fresh(kind + q, half), made["n3" + q][:], y[d, r][:, cols], ALU.subtract)
-            elif kind == "e2" or kind == "e3":
-                nc.scalar.activation(fresh(kind + q, half), made["s" + kind[1] + q][:], ACT.Exp, scale=minus_one[:])
-            elif kind == "U":
-                for j in range(4):
-                    src = made[f"neg{j // 2}_{r}"][:, h * half + j % 2 * P : h * half + (j % 2 + 1) * P]
-                    nc.tensor.matmul(
-                        bank[:, j * P : (j + 1) * P], src, ident[:], start=j == 0, stop=False, is_transpose=True
-                    )
-            elif kind == "T":
-                for j in range(4):
-                    top = made["n3" + q][:, j % 2 * P : (j % 2 + 1) * P]
-                    nc.tensor.matmul(
-                        bank[:, j * P : (j + 1) * P], top, ident[:], start=False, stop=j == 3, is_transpose=True
-                    )
-            elif kind == "eP":
-                nc.scalar.activation(fresh("eP" + q, V), bank[:], ACT.Exp, scale=minus_one[:])
-            elif kind == "B":
-                for b in range(2):
-                    for d in range(2):
-                        src = made["eP" + q][:, (2 * d + b) * P : (2 * d + b + 1) * P]
-                        nc.tensor.matmul(
-                            bank[:, b * P : (b + 1) * P], src, ident[:], start=d == 0, stop=d == 1, is_transpose=True
-                        )
-            elif kind == "a1":
-                made["a1" + q] = pair_sums[:, (2 * r + h) * half : (2 * r + h + 1) * half]
-                nc.vector.tensor_tensor(made["a1" + q], made["e2" + q][:], made["e3" + q][:], ALU.add)
-            else:
-                nc.vector.tensor_tensor(fresh("a2" + q, half), bank[:, :half], made["a1" + q][:], ALU.add)
+        def running_max(d):
+            return lambda r, h: nc.vector.tensor_tensor(
+                fresh(f"max{d}", r, h, HALF), scores(d, r, h), made[f"max{d - 1}", r, h], ALU.max
+            )
 
-        for item in ORDER.split():
-            kind, where = item.split("_")
-            step(kind, int_of[where[0]], int_of[where[1]])
+        def gap(d):
+            return lambda r, h: nc.vector.tensor_tensor(
+                fresh(f"gap{d}", r, h, HALF), made["max3", r, h], scores(d, r, h), ALU.subtract
+            )
+
+        def exp_of_gap(d):
+            return lambda r, h: nc.scalar.activation(
+                fresh(f"exp{d}", r, h, HALF), made[f"gap{d}", r, h], ACT.Exp, scale=minus_one[:]
+            )
+
+        def turn_scores(r, h):
+            for j in range(4):
+                first = r * HALF + j % 2 * P
+                src = made["negated", j // 2, h][:, first : first + P]
+                turn(made["bank", r, h][:, j * P : (j + 1) * P], src, j == 0, False)
+
+        def turn_max(r, h):
+            for j in range(4):
+                src = made["max3", r, h][:, j % 2 * P : (j % 2 + 1) * P]
+                turn(made["bank", r, h][:, j * P : (j + 1) * P], src, False, j == 3)
+
+        def exp01(r, h):
+            nc.scalar.activation(fresh("exp01", r, h, V), made["bank", r, h], ACT.Exp, scale=minus_one[:])
+
+        def sum01(r, h):
+            for b in range(2):
+                for d in range(2):
+                    src = made["exp01", r, h][:, (2 * d + b) * P : (2 * d + b + 1) * P]
+                    turn(made["bank", r, h][:, b * P : (b + 1) * P], src, d == 0, d == 1)
+
+        def sum23(r, h):
+            made["sum23", r, h] = sums23[:, (2 * r + h) * HALF : (2 * r + h + 1) * HALF]
+            nc.vector.tensor_tensor(made["sum23", r, h], made["exp2", r, h], made["exp3", r, h], ALU.add)
+
+        def total(r, h):
+            nc.vector.tensor_tensor(fresh("total", r, h, HALF), made["bank", r, h][:, :HALF], made["sum23", r, h], ALU.add)
+
+        steps = {
+            "gather": lambda d: gather_pair(1, d),
+            "weave": weave,
+            "quantise": quantise,
+            "score": score,
+            "negate": negate,
+            "max1": max1,
+            "max2": running_max(2),
+            "max3": running_max(3),
+            "gap2": gap(2),
+            "gap3": gap(3),
+            "exp2": exp_of_gap(2),
+            "exp3": exp_of_gap(3),
+            "turn_scores": turn_scores,
+            "turn_max": turn_max,
+            "exp01": exp01,
+            "sum01": sum01,
+            "sum23": sum23,
+            "total": total,
+        }
+        for step in STEPS.split():
+            name, digits = step.split(":")
+            steps[name](*[int(digit) for digit in digits])
 
         logged = keep.tile([P, ROW_TILES * V], F32, name="logged", tag="exp_then_ln")
         result = keep.tile([P, ROW_TILES * V], F32, name="result", tag="sums_then_results")
-        c0 = 0
-        for width in OUT_WIDTHS:
-            r, h, inner = c0 // V, c0 % V // half, slice(c0 % half, c0 % half + width)
-            q = f"{r}{h}"
-            nc.scalar.activation(logged[:, c0 : c0 + width], made["a2" + q][:, inner], ACT.Ln)
-            nc.vector.tensor_tensor(
-                result[:, c0 : c0 + width], logged[:, c0 : c0 + width], made["n3" + q][:, inner], ALU.add
-            )
-            nc.sync.dma_start(
-                out=out[r * P : (r + 1) * P, c0 % V : c0 % V + width], in_=result[:, c0 : c0 + width]
-            )
-            c0 += width
+        for r, h, first, width in STORES:
+            inner = slice(first, first + width)
+            place = h * HALF + first
+            cols = slice(r * V + place, r * V + place + width)
+            nc.scalar.activation(logged[:, cols], made["total", r, h][:, inner], ACT.Ln)
+            nc.vector.tensor_tensor(result[:, cols], logged[:, cols], made["max3", r, h][:, inner], ALU.add)
+            nc.sync.dma_start(out=out[r * P : (r + 1) * P, place : place + width], in_=result[:, cols])

from contextlib import ExitStack

import concourse.mybir as mybir
from concourse.masks import make_identity

K, T, S, V, N = 512, 4096, 2048, 512, 256
FLOPS = 2 * K * N * S

F32 = mybir.dt.float32
BF16 = mybir.dt.bfloat16
I32 = mybir.dt.int32
U32 = mybir.dt.uint32
U16 = mybir.dt.uint16
U8 = mybir.dt.uint8
FP8X4 = mybir.dt.float8_e4m3fn_x4
ALU = mybir.AluOpType
ACT = mybir.ActivationFunctionType

P = 128
PACK = 4
PIECES = S // V
ROW_TILES = N // P
HALF = V // 2
LIST_COLS = V // 16

LOADS = (
    ((3072, 1280), (1024, 384)),
    ((1536, 1536), (1536, 512), (512, 192), (512, 160)),
)

STEPS = """
gather:0 weave:00 weave:01 gather:1 weave:10 weave:11 gather:2 weave:20 weave:21 quantise:00 score:00
quantise:01 score:01 quantise:10 score:10 quantise:11 score:11 negate:00 gather:3 weave:30 weave:31
quantise:20 score:20 quantise:21 score:21 max1:00 max1:10 negate:10 quantise:30 score:30 max2:00
quantise:31 score:31 max2:10 negate:01 negate:11 max3:00 max3:10 gap2:00 exp2:00 gap2:10 exp2:10 max1:01
gap3:00 exp3:00 max2:01 max1:11 turn_scores:00 turn_scores:10 turn_max:00 exp01:00 turn_max:10 exp01:10
max3:01 gap3:10 exp3:10 max2:11 gap2:01 exp2:01 turn_scores:01 turn_max:01 exp01:01 turn_scores:11
max3:11 gap3:01 exp3:01 sum01:00 sum01:10 gap2:11 exp2:11 gap3:11 turn_max:11 exp01:11 exp3:11 sum23:00
sum23:10 total:00 sum01:01 sum01:11 sum23:01 total:10 sum23:11 total:01 total:11
"""

STORES = ((0, 0, 0, HALF), (1, 0, 0, HALF), (0, 1, 0, HALF), (1, 1, 0, P), (1, 1, P, P))


def tile_picked_lsep_none_e_kernel(tc, xT, w1_words, w1_scales, offs, out):
    nc = tc.nc
    with ExitStack() as ctx:
        keep = ctx.enter_context(tc.tile_pool(name="keep", bufs=1))
        psum = ctx.enter_context(tc.psum_pool(name="psum", bufs=1))

        offsets = keep.tile([P, S // 16], U16, name="offsets")
        w_codes = keep.tile([P, N], U32, name="w_codes", align_bytes=64)
        w_scales = keep.tile([P, N], U8, name="w_scales", align_bytes=64)
        nc.gpsimd.memset(w_scales[:], 0)
        ident = keep.tile([P, P], F32, name="ident")
        make_identity(nc, ident[:])

        shared = keep.tile([P, 3, V], U32, name="picked13")
        picked = {1: shared[:, 1:3, :], 3: shared[:, 0:2, :]}
        for d in (0, 2):
            picked[d] = keep.tile([P, 2, V], U32, name=f"picked{d}")[:]

        def gather_pair(u, d):
            entries = offsets[:, d * LIST_COLS : (d + 1) * LIST_COLS]
            nc.vector.tensor_copy(picked[d][:, u, :], windows[u][:].bitcast(U32).indirect(entries))

        x_rows = xT.rearrange("(p j) t -> p j t", j=PACK)
        windows = []
        for u in range(2):
            windows.append(keep.tile([P, 2 * T], BF16, name=f"window{u}", align_bytes=64))
            pairs = windows[u][:].rearrange("p (t e) -> p t e", e=2)
            t0 = 0
            for c, (width, on_scalar) in enumerate(LOADS[u]):
                raw = keep.tile([P, 2, width], F32, name=f"raw{u}_{c}")
                nc.sync.dma_start(out=raw[:], in_=x_rows[:, 2 * u : 2 * u + 2, t0 : t0 + width])
                by_token = raw[:].rearrange("p e t -> p t e")
                nc.scalar.activation(pairs[:, t0 : t0 + on_scalar, :], by_token[:, :on_scalar, :], ACT.Copy)
                if on_scalar < width:
                    nc.vector.tensor_copy(pairs[:, t0 + on_scalar : t0 + width, :], by_token[:, on_scalar:, :])
                t0 += width
            if u == 0:
                nc.sync.dma_start(offsets[:], offs)
                for d in range(PIECES):
                    gather_pair(0, d)

        nc.sync.dma_start(out=w_codes[:].bitcast(I32), in_=w1_words[0].rearrange("p n t -> p (n t)").bitcast(I32))
        for q in range(4):
            nc.sync.dma_start(
                out=w_scales[32 * q : 32 * q + 4, :].bitcast(I32), in_=w1_scales[0, 4 * q : 4 * q + 4, :].bitcast(I32)
            )

        minus_one = keep.tile([P, 1], F32, name="minus_one", tag="exp_then_ln")
        nc.gpsimd.memset(minus_one[:], -1.0)
        sums23 = keep.tile([P, ROW_TILES * V], F32, name="sums23", tag="sums_then_results")

        made = {}

        def fresh(name, i, j, width, dtype=F32):
            made[name, i, j] = keep.tile([P, width], dtype, name=f"{name}_{i}{j}", align_bytes=64)[:]
            return made[name, i, j]

        def scores(d, r, h):
            return made["bank", d, h][:, r * HALF : (r + 1) * HALF]

        def turn(to, src, start, stop):
            nc.tensor.matmul(to, src, ident[:], start=start, stop=stop, is_transpose=True)

        def weave(d, h):
            woven = fresh("woven", d, h, PACK * HALF, BF16).bitcast(U32).rearrange("p (n u) -> p n u", u=2)
            nc.scalar.copy(woven, picked[d][:, :, h * HALF : (h + 1) * HALF].rearrange("p u n -> p n u"))

        def quantise(d, h):
            codes = fresh("codes", d, h, HALF, U32)
            nc.vector.quantize_mx(out=codes.bitcast(FP8X4), scales=fresh("scales", d, h, HALF, U8), in_=made["woven", d, h])

        def score(d, h):
            made["bank", d, h] = psum.tile([P, V], F32, name=f"bank{d}{h}")[:]
            for r in range(ROW_TILES):
                nc.tensor.matmul_mx(
                    out=scores(d, r, h),
                    lhsT=w_codes[:, r * P : (r + 1) * P].bitcast(FP8X4),
                    lhsT_scale=w_scales[:, r * P : (r + 1) * P],
                    rhs=made["codes", d, h].bitcast(FP8X4),
                    rhs_scale=made["scales", d, h],
                    start=True,
                    stop=True,
                )

        def negate(d, h):
            nc.scalar.activation(fresh("negated", d, h, V), made["bank", d, h], ACT.Copy, scale=-1.0)

        def max1(r, h):
            minus_y0 = made["negated", 0, h][:, r * HALF : (r + 1) * HALF]
            nc.vector.scalar_tensor_tensor(fresh("max1", r, h, HALF), minus_y0, -1.0, scores(1, r, h), ALU.mult, ALU.max)

        def running_max(d):
            return lambda r, h: nc.vector.tensor_tensor(
                fresh(f"max{d}", r, h, HALF), scores(d, r, h), made[f"max{d - 1}", r, h], ALU.max
            )

        def gap(d):
            return lambda r, h: nc.vector.tensor_tensor(
                fresh(f"gap{d}", r, h, HALF), made["max3", r, h], scores(d, r, h), ALU.subtract
            )

        def exp_of_gap(d):
            return lambda r, h: nc.scalar.activation(
                fresh(f"exp{d}", r, h, HALF), made[f"gap{d}", r, h], ACT.Exp, scale=minus_one[:]
            )

        def turn_scores(r, h):
            for j in range(4):
                first = r * HALF + j % 2 * P
                src = made["negated", j // 2, h][:, first : first + P]
                turn(made["bank", r, h][:, j * P : (j + 1) * P], src, j == 0, False)

        def turn_max(r, h):
            for j in range(4):
                src = made["max3", r, h][:, j % 2 * P : (j % 2 + 1) * P]
                turn(made["bank", r, h][:, j * P : (j + 1) * P], src, False, j == 3)

        def exp01(r, h):
            nc.scalar.activation(fresh("exp01", r, h, V), made["bank", r, h], ACT.Exp, scale=minus_one[:])

        def sum01(r, h):
            for b in range(2):
                for d in range(2):
                    src = made["exp01", r, h][:, (2 * d + b) * P : (2 * d + b + 1) * P]
                    turn(made["bank", r, h][:, b * P : (b + 1) * P], src, d == 0, d == 1)

        def sum23(r, h):
            made["sum23", r, h] = sums23[:, (2 * r + h) * HALF : (2 * r + h + 1) * HALF]
            nc.vector.tensor_tensor(made["sum23", r, h], made["exp2", r, h], made["exp3", r, h], ALU.add)

        def total(r, h):
            nc.vector.tensor_tensor(fresh("total", r, h, HALF), made["bank", r, h][:, :HALF], made["sum23", r, h], ALU.add)

        steps = {
            "gather": lambda d: gather_pair(1, d),
            "weave": weave,
            "quantise": quantise,
            "score": score,
            "negate": negate,
            "max1": max1,
            "max2": running_max(2),
            "max3": running_max(3),
            "gap2": gap(2),
            "gap3": gap(3),
            "exp2": exp_of_gap(2),
            "exp3": exp_of_gap(3),
            "turn_scores": turn_scores,
            "turn_max": turn_max,
            "exp01": exp01,
            "sum01": sum01,
            "sum23": sum23,
            "total": total,
        }
        for step in STEPS.split():
            name, digits = step.split(":")
            steps[name](*[int(digit) for digit in digits])

        logged = keep.tile([P, ROW_TILES * V], F32, name="logged", tag="exp_then_ln")
        result = keep.tile([P, ROW_TILES * V], F32, name="result", tag="sums_then_results")
        for r, h, first, width in STORES:
            inner = slice(first, first + width)
            place = h * HALF + first
            cols = slice(r * V + place, r * V + place + width)
            nc.scalar.activation(logged[:, cols], made["total", r, h][:, inner], ACT.Ln)
            nc.vector.tensor_tensor(result[:, cols], logged[:, cols], made["max3", r, h][:, inner], ALU.add)
            nc.sync.dma_start(out=out[r * P : (r + 1) * P, place : place + width], in_=result[:, cols])
